import numpy as np
import ml_dtypes


def mxq(x, axis, fmt="e4m3"):
    dtype, down = {"e4m3": (ml_dtypes.float8_e4m3fn, 7), "e5m2": (ml_dtypes.float8_e5m2, 14)}[fmt]
    v = np.moveaxis(np.asarray(x, np.float32).astype(ml_dtypes.bfloat16).astype(np.float64), axis, -1)
    blocks = v.reshape(v.shape[:-1] + (-1, 32))
    amax = np.abs(blocks).max(-1, keepdims=True)
    byte = np.maximum(np.where(amax > 0, np.frexp(amax)[1] - 1 + 127, 0) - down, 1)
    scale = np.exp2(byte - 127.0)
    codes = (blocks / scale).astype(np.float32).astype(dtype).astype(np.float64)
    return np.moveaxis((codes * scale).reshape(v.shape), -1, axis)


WIDE = False


def mx_kscale(k):
    if not WIDE:
        return np.ones(k)
    levels = np.array([10, -10, 5, -5, 0])
    if k % 512:
        return np.exp2(np.random.permutation(np.resize(levels, k // 32))).repeat(32)
    a = np.empty((k // 512, 16))
    for p in range(k // 512):
        a[p, :8] = np.random.permutation(np.resize(levels, 8))
        for g in range(8):
            far = levels[np.abs(levels - a[p, g]) >= 10]
            a[p, g + 8] = far[np.random.randint(len(far))]
    return np.exp2(a.ravel()).repeat(32)


def f64(x):
    return np.asarray(x).astype(np.float64)


def striped(idx):
    return np.tile(idx.reshape(-1, 16).T, (8, 1)).astype(np.uint16)


def unstriped(offs):
    return offs[:16].T.reshape(-1).astype(np.int64)


def relu(v):
    return np.maximum(v, 0.0)


K, T, E, C, H, N = 1024, 1024, 4, 128, 512, 512


def by_expert(wq, xq):
    return np.concatenate([wq[e].T @ xq[:, e * C:(e + 1) * C] for e in range(E)], axis=1)


def setup_inputs():
    n = np.random.standard_normal
    s = mx_kscale(K)[:, None]
    u = mx_kscale(H)
    return {
        "xT": (n((K, T)) * s).astype(np.float32),
        "xr": n((N, T)).astype(np.float32),
        "w1": (n((E, K, H)) / np.sqrt(K) / s[None] * u[None, None, :]).astype(np.float32),
        "w2": (n((E, H, N)) / np.sqrt(H) / u[None, :, None]).astype(np.float32),
        "gate": np.tile(np.random.uniform(0.2, 1.0, E * C), (N, 1)).astype(np.float32),
        "offs": striped(np.random.permutation(T)[:E * C]),
    }


def reference(xT, xr, w1, w2, gate, offs):
    idx = unstriped(offs)
    xq = mxq(f64(xT)[:, idx], 0, "e4m3")
    h = relu(by_expert(mxq(f64(w1), 1, "e4m3"), xq))
    y = by_expert(mxq(f64(w2), 1, "e4m3"), mxq(h, 0, "e4m3"))
    out = f64(xr).copy()
    out[:, idx] += f64(gate) * y
    return out

@@ -1,0 +1,220 @@
+from contextlib import ExitStack
+
+import concourse.mybir as mybir
+
+K, T, E, C, H, N = 1024, 1024, 4, 128, 512, 512
+S = E * C
+FLOPS = 2 * S * (K * H + H * N)
+
+F32 = mybir.dt.float32
+BF16 = mybir.dt.bfloat16
+U32 = mybir.dt.uint32
+U16 = mybir.dt.uint16
+U8 = mybir.dt.uint8
+FP8X4 = mybir.dt.float8_e4m3fn_x4
+ADD = mybir.AluOpType.add
+MULT = mybir.AluOpType.mult
+RELU = mybir.ActivationFunctionType.Relu
+
+P = 128
+J = 4
+KP = P * J
+PASSES = K // KP
+NT = N // P
+
+
+def tile_moe_res_mlp_relu_kernel(tc, xT, xr, w1, w2, gate, offs, out):
+    nc = tc.nc
+    with ExitStack() as ctx:
+        keep = ctx.enter_context(tc.tile_pool(name="keep", bufs=1))
+        raws = ctx.enter_context(tc.tile_pool(name="raws", bufs=16))
+        stage = ctx.enter_context(tc.tile_pool(name="stage", bufs=4))
+        work = ctx.enter_context(tc.tile_pool(name="work", bufs=2))
+        psum = ctx.enter_context(tc.psum_pool(name="psum", bufs=2))
+
+        offsets = keep.tile([P, S // 16], U16, name="offsets")
+        gates = keep.tile([P, S], F32, name="gates")
+        x_codes = [keep.tile([P, T], U32, name=f"x_codes{s}", align_bytes=64) for s in range(PASSES)]
+        x_scales = [keep.tile([P, T], U8, name=f"x_scales{s}", align_bytes=64) for s in range(PASSES)]
+        g_codes = [keep.tile([P, S], U32, name=f"g_codes{s}", align_bytes=64) for s in range(PASSES)]
+        g_scales = [keep.tile([P, S], U8, name=f"g_scales{s}", align_bytes=64) for s in range(PASSES)]
+        w1_codes = [[keep.tile([P, H], U32, name=f"w1_codes{e}_{s}", align_bytes=64) for s in range(PASSES)] for e in range(E)]
+        w1_scales = [[keep.tile([P, H], U8, name=f"w1_scales{e}_{s}", align_bytes=64) for s in range(PASSES)] for e in range(E)]
+        w2_codes = [keep.tile([P, N], U32, name=f"w2_codes{e}", align_bytes=64) for e in range(E)]
+        w2_scales = [keep.tile([P, N], U8, name=f"w2_scales{e}", align_bytes=64) for e in range(E)]
+        windows = [keep.tile([P, T], F32, name=f"window{n}") for n in range(NT)]
+        res = [keep.tile([P, T], F32, name=f"res{n}") for n in range(NT)]
+
+        for s in range(PASSES):
+            nc.gpsimd.memset(x_scales[s][:], 0)
+        for n in range(NT):
+            nc.gpsimd.memset(windows[n][:], 0.0)
+
+        def load(source):
+            raw = raws.tile([P, J, 512], F32, name="raw")
+            nc.sync.dma_start(out=raw[:], in_=source.rearrange("(p j) c -> p j c", j=J))
+            return raw
+
+        def load_x(s, half):
+            return load(xT[s * KP : (s + 1) * KP, half * 512 : (half + 1) * 512])
+
+        def load_w1(e, s):
+            return load(w1[e][s * KP : (s + 1) * KP, :])
+
+        def load_w2(e):
+            return load(w2[e])
+
+        def group(copy, raw, grouped, lo=0, hi=512):
+            copy(
+                out=grouped[:].rearrange("p (c j) -> p c j", j=J)[:, lo:hi, :].rearrange("p (c i) j -> p c j i", i=4),
+                in_=raw[:, :, lo:hi].rearrange("p j (c i) -> p c j i", i=4),
+            )
+
+        def group_turned(copy, raw, grouped, lo=0, hi=P):
+            copy(
+                out=grouped[:].rearrange("p (t m j) -> p m j t", t=4, j=J)[:, lo:hi],
+                in_=raw[:].rearrange("p j (m t) -> p m j t", t=4)[:, lo:hi],
+            )
+
+        def new_grouped():
+            grouped = stage.tile([P, 512 * J], BF16, name="grouped", align_bytes=64)
+            return grouped
+
+        def quantise(grouped, codes, scales):
+            nc.vector.quantize_mx(out=codes.bitcast(FP8X4), scales=scales, in_=grouped[:])
+
+        def copy_x(s, half, raw):
+            grouped = new_grouped()
+            group(nc.scalar.copy, raw, grouped, 0, 256)
+            group(nc.vector.tensor_copy, raw, grouped, 256, 512)
+            return grouped
+
+        def quant_x(s, half, grouped):
+            cols = slice(half * 512, (half + 1) * 512)
+            quantise(grouped, x_codes[s][:, cols], x_scales[s][:, cols])
+
+        def gather(s):
+            nc.vector.tensor_copy(g_codes[s][:], x_codes[s][:].indirect(offsets[:]))
+            nc.vector.tensor_copy(g_scales[s][:], x_scales[s][:].indirect(offsets[:]))
+
+        def copy_w1(e, s, raw, share):
+            grouped = new_grouped()
+            group_turned(nc.scalar.copy, raw, grouped, share // 4, P)
+            group_turned(nc.vector.tensor_copy, raw, grouped, 0, share // 4)
+            return grouped
+
+        def quant_w1(e, s, grouped):
+            quantise(grouped, w1_codes[e][s][:], w1_scales[e][s][:])
+
+        def copy_w2(e, raw, share):
+            grouped = new_grouped()
+            group(nc.scalar.copy, raw, grouped, share, 512)
+            group(nc.vector.tensor_copy, raw, grouped, 0, share)
+            return grouped
+
+        def quant_w2(e, grouped):
+            quantise(grouped, w2_codes[e][:], w2_scales[e][:])
+
+        def layer1(e):
+            slots = slice(e * C, (e + 1) * C)
+            acc = psum.tile([P, 4, C], F32, name="acc1")
+            for t in range(4):
+                rows = slice(t * P, (t + 1) * P)
+                for s in range(PASSES):
+                    nc.tensor.matmul_mx(
+                        out=acc[:, t, :],
+                        lhsT=w1_codes[e][s][:, rows].bitcast(FP8X4),
+                        lhsT_scale=w1_scales[e][s][:, rows],
+                        rhs=g_codes[s][:, slots].bitcast(FP8X4),
+                        rhs_scale=g_scales[s][:, slots],
+                        start=(s == 0),
+                        stop=(s == PASSES - 1),
+                    )
+            hidden = work.tile([P, C * J], BF16, name="hidden", align_bytes=64)
+            nc.scalar.activation(
+                out=hidden[:].rearrange("p (c t) -> p c t", t=4),
+                in_=acc[:].rearrange("p t c -> p c t"),
+                func=RELU,
+            )
+            h_codes = work.tile([P, C], U32, name="h_codes", align_bytes=64)
+            h_scales = work.tile([P, C], U8, name="h_scales", align_bytes=64)
+            nc.vector.quantize_mx(out=h_codes[:].bitcast(FP8X4), scales=h_scales[:], in_=hidden[:])
+            return h_codes, h_scales
+
+        def layer2(e, h):
+            h_codes, h_scales = h
+            acc = psum.tile([P, NT, C], F32, name="acc2")
+            for n in range(NT):
+                rows = slice(n * P, (n + 1) * P)
+                nc.tensor.matmul_mx(
+                    out=acc[:, n, :],
+                    lhsT=w2_codes[e][:, rows].bitcast(FP8X4),
+                    lhsT_scale=w2_scales[e][:, rows],
+                    rhs=h_codes[:].bitcast(FP8X4),
+                    rhs_scale=h_scales[:],
+                    start=True,
+                    stop=True,
+                )
+            y = work.tile([P, NT, C], F32, name="y")
+            nc.scalar.copy(out=y[:], in_=acc[:])
+            return y
+
+        def scatter(e, n, y):
+            nc.vector.tensor_tensor(
+                windows[n][:].indirect(offsets[:, e * (C // 16) : (e + 1) * (C // 16)]),
+                y[:, n, :],
+                gates[:, e * C : (e + 1) * C],
+                MULT,
+            )
+
+        nc.sync.dma_start(offsets[:], offs)
+        r_x = [[None, None], [None, None]]
+        r_a = [[None, None] for e in range(E)]
+        r_b = [None for e in range(E)]
+        r_x[0][0] = load_x(0, 0)
+        r_x[0][1] = load_x(0, 1)
+        r_a[0][0] = load_w1(0, 0)
+        r_x[1][0] = load_x(1, 0)
+        r_x[1][1] = load_x(1, 1)
+        r_a[0][1] = load_w1(0, 1)
+        r_b[0] = load_w2(0)
+        nc.sync.dma_start(out=gates[:], in_=gate[0:P, :])
+        for e in range(1, E):
+            r_a[e][0] = load_w1(e, 0)
+            r_a[e][1] = load_w1(e, 1)
+            r_b[e] = load_w2(e)
+        for n in range(NT):
+            rows = slice(n * P, (n + 1) * P)
+            nc.sync.dma_start(out=res[n][:], in_=xr[rows, :])
+
+        share = [192, 192, 192, 128]
+        for s in range(PASSES):
+            left = copy_x(s, 0, r_x[s][0])
+            right = copy_x(s, 1, r_x[s][1])
+            quant_x(s, 0, left)
+            grouped = copy_w1(0, s, r_a[0][s], share[0])
+            quant_x(s, 1, right)
+            gather(s)
+            quant_w1(0, s, grouped)
+
+        y = None
+        for e in range(E):
+            h = None
+            g_b = copy_w2(e, r_b[e], share[e])
+            if e < E - 1:
+                g_a = copy_w1(e + 1, 0, r_a[e + 1][0], share[e + 1])
+            quant_w2(e, g_b)
+            h = layer1(e)
+            if e < E - 1:
+                quant_w1(e + 1, 0, g_a)
+                g_a = copy_w1(e + 1, 1, r_a[e + 1][1], share[e + 1])
+            y = layer2(e, h)
+            if e < E - 1:
+                quant_w1(e + 1, 1, g_a)
+                for n in range(NT):
+                    scatter(e, n, y)
+        for n in range(NT):
+            rows = slice(n * P, (n + 1) * P)
+            scatter(E - 1, n, y)
+            nc.vector.tensor_tensor(res[n][:], windows[n][:], res[n][:], ADD)
+            nc.sync.dma_start(out=out[rows, :], in_=res[n][:])

@@ -27,17 +27,18 @@ def tile_moe_res_mlp_relu_kernel(tc, xT, xr, w1, w2, gate, offs, out):
     nc = tc.nc
     with ExitStack() as ctx:
         keep = ctx.enter_context(tc.tile_pool(name="keep", bufs=1))
-        raws = ctx.enter_context(tc.tile_pool(name="raws", bufs=16))
-        stage = ctx.enter_context(tc.tile_pool(name="stage", bufs=4))
+        raws = ctx.enter_context(tc.tile_pool(name="raws", bufs=14))
+        stage = ctx.enter_context(tc.tile_pool(name="stage", bufs=5))
         work = ctx.enter_context(tc.tile_pool(name="work", bufs=2))
+        ys = ctx.enter_context(tc.tile_pool(name="ys", bufs=4))
         psum = ctx.enter_context(tc.psum_pool(name="psum", bufs=2))
 
         offsets = keep.tile([P, S // 16], U16, name="offsets")
         gates = keep.tile([P, S], F32, name="gates")
         x_codes = [keep.tile([P, T], U32, name=f"x_codes{s}", align_bytes=64) for s in range(PASSES)]
-        x_scales = [keep.tile([P, T], U8, name=f"x_scales{s}", align_bytes=64) for s in range(PASSES)]
+        x_scales = keep.tile([P, T], U8, name="x_scales", align_bytes=64)
         g_codes = [keep.tile([P, S], U32, name=f"g_codes{s}", align_bytes=64) for s in range(PASSES)]
-        g_scales = [keep.tile([P, S], U8, name=f"g_scales{s}", align_bytes=64) for s in range(PASSES)]
+        g_scales = keep.tile([P, S], U8, name="g_scales", align_bytes=64)
         w1_codes = [[keep.tile([P, H], U32, name=f"w1_codes{e}_{s}", align_bytes=64) for s in range(PASSES)] for e in range(E)]
         w1_scales = [[keep.tile([P, H], U8, name=f"w1_scales{e}_{s}", align_bytes=64) for s in range(PASSES)] for e in range(E)]
         w2_codes = [keep.tile([P, N], U32, name=f"w2_codes{e}", align_bytes=64) for e in range(E)]
@@ -45,10 +46,9 @@ def tile_moe_res_mlp_relu_kernel(tc, xT, xr, w1, w2, gate, offs, out):
         windows = [keep.tile([P, T], F32, name=f"window{n}") for n in range(NT)]
         res = [keep.tile([P, T], F32, name=f"res{n}") for n in range(NT)]
 
-        for s in range(PASSES):
-            nc.gpsimd.memset(x_scales[s][:], 0)
+        nc.gpsimd.memset(x_scales[:], 0)
         for n in range(NT):
-            nc.gpsimd.memset(windows[n][:], 0.0)
+            nc.vector.memset(windows[n][:], 0.0)
 
         def load(source):
             raw = raws.tile([P, J, 512], F32, name="raw")
@@ -63,6 +63,20 @@ def tile_moe_res_mlp_relu_kernel(tc, xT, xr, w1, w2, gate, offs, out):
 
         def load_w2(e):
             return load(w2[e])
+
+        def load_half_w2(e, half):
+            raw = raws.tile([P, J, 256], F32, name="raw")
+            nc.sync.dma_start(out=raw[:], in_=w2[e][:, half * 256 : (half + 1) * 256].rearrange("(p j) c -> p j c", j=J))
+            return raw
+
+        def do_half_w2(e, half, raw):
+            grouped = stage.tile([P, 256 * J], BF16, name="grouped", align_bytes=64)
+            nc.scalar.copy(
+                out=grouped[:].rearrange("p (c i j) -> p c j i", i=4, j=J),
+                in_=raw[:].rearrange("p j (c i) -> p c j i", i=4),
+            )
+            cols = slice(half * 256, (half + 1) * 256)
+            quantise(grouped, w2_codes[e][:, cols], w2_scales[e][:, cols])
 
         def group(copy, raw, grouped, lo=0, hi=512):
             copy(
@@ -91,28 +105,26 @@ def tile_moe_res_mlp_relu_kernel(tc, xT, xr, w1, w2, gate, offs, out):
 
         def quant_x(s, half, grouped):
             cols = slice(half * 512, (half + 1) * 512)
-            quantise(grouped, x_codes[s][:, cols], x_scales[s][:, cols])
+            quantise(grouped, x_codes[s][:, cols], x_scales[4 * s : P, cols])
 
         def gather(s):
             nc.vector.tensor_copy(g_codes[s][:], x_codes[s][:].indirect(offsets[:]))
-            nc.vector.tensor_copy(g_scales[s][:], x_scales[s][:].indirect(offsets[:]))
 
-        def copy_w1(e, s, raw, share):
+        def copy_w1(e, s, raw):
             grouped = new_grouped()
-            group_turned(nc.scalar.copy, raw, grouped, share // 4, P)
-            group_turned(nc.vector.tensor_copy, raw, grouped, 0, share // 4)
+            if s == 0:
+                group_turned(nc.scalar.copy, raw, grouped)
+            else:
+                group_turned(nc.scalar.copy, raw, grouped, 0, P // 2)
+                group_turned(nc.vector.tensor_copy, raw, grouped, P // 2, P)
             return grouped
 
         def quant_w1(e, s, grouped):
             quantise(grouped, w1_codes[e][s][:], w1_scales[e][s][:])
 
-        def copy_w2(e, raw, share):
+        def do_w2(e, raw):
             grouped = new_grouped()
-            group(nc.scalar.copy, raw, grouped, share, 512)
-            group(nc.vector.tensor_copy, raw, grouped, 0, share)
-            return grouped
-
-        def quant_w2(e, grouped):
+            group(nc.scalar.copy, raw, grouped)
             quantise(grouped, w2_codes[e][:], w2_scales[e][:])
 
         def layer1(e):
@@ -126,7 +138,7 @@ def tile_moe_res_mlp_relu_kernel(tc, xT, xr, w1, w2, gate, offs, out):
                         lhsT=w1_codes[e][s][:, rows].bitcast(FP8X4),
                         lhsT_scale=w1_scales[e][s][:, rows],
                         rhs=g_codes[s][:, slots].bitcast(FP8X4),
-                        rhs_scale=g_scales[s][:, slots],
+                        rhs_scale=g_scales[4 * s : P, slots],
                         start=(s == 0),
                         stop=(s == PASSES - 1),
                     )
@@ -141,13 +153,13 @@ def tile_moe_res_mlp_relu_kernel(tc, xT, xr, w1, w2, gate, offs, out):
             nc.vector.quantize_mx(out=h_codes[:].bitcast(FP8X4), scales=h_scales[:], in_=hidden[:])
             return h_codes, h_scales
 
-        def layer2(e, h):
+        def layer2(e, h, tiles=range(NT)):
             h_codes, h_scales = h
-            acc = psum.tile([P, NT, C], F32, name="acc2")
-            for n in range(NT):
+            acc = psum.tile([P, len(tiles), C], F32, name="acc2")
+            for i, n in enumerate(tiles):
                 rows = slice(n * P, (n + 1) * P)
                 nc.tensor.matmul_mx(
-                    out=acc[:, n, :],
+                    out=acc[:, i, :],
                     lhsT=w2_codes[e][:, rows].bitcast(FP8X4),
                     lhsT_scale=w2_scales[e][:, rows],
                     rhs=h_codes[:].bitcast(FP8X4),
@@ -155,66 +167,71 @@ def tile_moe_res_mlp_relu_kernel(tc, xT, xr, w1, w2, gate, offs, out):
                     start=True,
                     stop=True,
                 )
-            y = work.tile([P, NT, C], F32, name="y")
+            y = ys.tile([P, len(tiles), C], F32, name="y")
             nc.scalar.copy(out=y[:], in_=acc[:])
-            return y
+            return [y[:, i, :] for i in range(len(tiles))]
 
         def scatter(e, n, y):
             nc.vector.tensor_tensor(
                 windows[n][:].indirect(offsets[:, e * (C // 16) : (e + 1) * (C // 16)]),
-                y[:, n, :],
+                y,
                 gates[:, e * C : (e + 1) * C],
                 MULT,
             )
 
-        nc.sync.dma_start(offsets[:], offs)
         r_x = [[None, None], [None, None]]
         r_a = [[None, None] for e in range(E)]
         r_b = [None for e in range(E)]
         r_x[0][0] = load_x(0, 0)
         r_x[0][1] = load_x(0, 1)
-        r_a[0][0] = load_w1(0, 0)
+        nc.sync.dma_start(offsets[:], offs)
         r_x[1][0] = load_x(1, 0)
         r_x[1][1] = load_x(1, 1)
+        r_a[0][0] = load_w1(0, 0)
         r_a[0][1] = load_w1(0, 1)
         r_b[0] = load_w2(0)
         nc.sync.dma_start(out=gates[:], in_=gate[0:P, :])
         for e in range(1, E):
             r_a[e][0] = load_w1(e, 0)
             r_a[e][1] = load_w1(e, 1)
-            r_b[e] = load_w2(e)
+            if e < E - 1:
+                r_b[e] = load_w2(e)
+            else:
+                r_b[e] = [load_half_w2(e, half) for half in range(2)]
         for n in range(NT):
             rows = slice(n * P, (n + 1) * P)
             nc.sync.dma_start(out=res[n][:], in_=xr[rows, :])
 
-        share = [192, 192, 192, 128]
         for s in range(PASSES):
             left = copy_x(s, 0, r_x[s][0])
             right = copy_x(s, 1, r_x[s][1])
             quant_x(s, 0, left)
-            grouped = copy_w1(0, s, r_a[0][s], share[0])
             quant_x(s, 1, right)
             gather(s)
-            quant_w1(0, s, grouped)
+        nc.vector.tensor_copy(g_scales[:], x_scales[:].indirect(offsets[:]))
 
-        y = None
+        y = []
         for e in range(E):
-            h = None
-            g_b = copy_w2(e, r_b[e], share[e])
+            g_0 = copy_w1(e, 0, r_a[e][0])
+            g_1 = copy_w1(e, 1, r_a[e][1])
+            quant_w1(e, 0, g_0)
+            quant_w1(e, 1, g_1)
             if e < E - 1:
-                g_a = copy_w1(e + 1, 0, r_a[e + 1][0], share[e + 1])
-            quant_w2(e, g_b)
-            h = layer1(e)
-            if e < E - 1:
-                quant_w1(e + 1, 0, g_a)
-                g_a = copy_w1(e + 1, 1, r_a[e + 1][1], share[e + 1])
-            y = layer2(e, h)
-            if e < E - 1:
-                quant_w1(e + 1, 1, g_a)
+                do_w2(e, r_b[e])
+                y.append(layer2(e, layer1(e)))
+            else:
+                for half in range(2):
+                    do_half_w2(e, half, r_b[e][half])
+                h = layer1(e)
+                y.append(layer2(e, h, range(2)) + layer2(e, h, range(2, 4)))
+            if e >= 1:
                 for n in range(NT):
-                    scatter(e, n, y)
+                    scatter(e - 1, n, y[e - 1][n])
         for n in range(NT):
             rows = slice(n * P, (n + 1) * P)
-            scatter(E - 1, n, y)
-            nc.vector.tensor_tensor(res[n][:], windows[n][:], res[n][:], ADD)
-            nc.sync.dma_start(out=out[rows, :], in_=res[n][:])
+            scatter(E - 1, n, y[E - 1][n])
+            parts = 1 if n < NT - 1 else 2
+            for i in range(parts):
+                cols = slice(i * T // parts, (i + 1) * T // parts)
+                nc.vector.tensor_tensor(res[n][:, cols], windows[n][:, cols], res[n][:, cols], ADD)
+                nc.sync.dma_start(out=out[rows, cols], in_=res[n][:, cols])

@@ -16,6 +16,8 @@ ADD = mybir.AluOpType.add
 MULT = mybir.AluOpType.mult
 RELU = mybir.ActivationFunctionType.Relu
 
+PARAMS = {"loads":["x01","o","x00","a01","x11","x10","a00","b0","a21","g","a31","b1","a10","a11","a20","b2","a30","b3R","b3L","r3","r2","r0","r1"],"share":{"x00":0.75,"x01":0.25,"x10":0.5,"x11":0.5,"a00":0,"a01":0.5,"b0":0.75,"a10":0.25,"a11":0.25,"b1":0.5,"a20":0.25,"a21":0.75,"b2":0.25,"a30":0,"a31":0,"b3L":0,"b3R":0.5},"raws":9,"stage":1,"lag":2,"quota":2,"experts":[0,1,2,3]}
+
 P = 128
 J = 4
 KP = P * J
@@ -27,11 +29,11 @@ def tile_moe_res_mlp_relu_kernel(tc, xT, xr, w1, w2, gate, offs, out):
     nc = tc.nc
     with ExitStack() as ctx:
         keep = ctx.enter_context(tc.tile_pool(name="keep", bufs=1))
-        raws = ctx.enter_context(tc.tile_pool(name="raws", bufs=14))
-        stage = ctx.enter_context(tc.tile_pool(name="stage", bufs=5))
-        work = ctx.enter_context(tc.tile_pool(name="work", bufs=2))
-        ys = ctx.enter_context(tc.tile_pool(name="ys", bufs=4))
-        psum = ctx.enter_context(tc.psum_pool(name="psum", bufs=2))
+        raws = ctx.enter_context(tc.tile_pool(name="raws", bufs=PARAMS["raws"]))
+        stage = ctx.enter_context(tc.tile_pool(name="stage", bufs=PARAMS["stage"]))
+        work = ctx.enter_context(tc.tile_pool(name="work", bufs=4))
+        ys = ctx.enter_context(tc.tile_pool(name="ys", bufs=5))
+        psum = ctx.enter_context(tc.psum_pool(name="psum", bufs=1))
 
         offsets = keep.tile([P, S // 16], U16, name="offsets")
         gates = keep.tile([P, S], F32, name="gates")
@@ -48,88 +50,61 @@ def tile_moe_res_mlp_relu_kernel(tc, xT, xr, w1, w2, gate, offs, out):
 
         nc.gpsimd.memset(x_scales[:], 0)
         for n in range(NT):
-            nc.vector.memset(windows[n][:], 0.0)
+            nc.gpsimd.memset(windows[n][:], 0.0)
 
-        def load(source):
-            raw = raws.tile([P, J, 512], F32, name="raw")
-            nc.sync.dma_start(out=raw[:], in_=source.rearrange("(p j) c -> p j c", j=J))
-            return raw
+        raw = {}
 
-        def load_x(s, half):
-            return load(xT[s * KP : (s + 1) * KP, half * 512 : (half + 1) * 512])
-
-        def load_w1(e, s):
-            return load(w1[e][s * KP : (s + 1) * KP, :])
-
-        def load_w2(e):
-            return load(w2[e])
-
-        def load_half_w2(e, half):
-            raw = raws.tile([P, J, 256], F32, name="raw")
-            nc.sync.dma_start(out=raw[:], in_=w2[e][:, half * 256 : (half + 1) * 256].rearrange("(p j) c -> p j c", j=J))
-            return raw
-
-        def do_half_w2(e, half, raw):
-            grouped = stage.tile([P, 256 * J], BF16, name="grouped", align_bytes=64)
-            nc.scalar.copy(
-                out=grouped[:].rearrange("p (c i j) -> p c j i", i=4, j=J),
-                in_=raw[:].rearrange("p j (c i) -> p c j i", i=4),
-            )
-            cols = slice(half * 256, (half + 1) * 256)
-            quantise(grouped, w2_codes[e][:, cols], w2_scales[e][:, cols])
-
-        def group(copy, raw, grouped, lo=0, hi=512):
-            copy(
-                out=grouped[:].rearrange("p (c j) -> p c j", j=J)[:, lo:hi, :].rearrange("p (c i) j -> p c j i", i=4),
-                in_=raw[:, :, lo:hi].rearrange("p j (c i) -> p c j i", i=4),
-            )
-
-        def group_turned(copy, raw, grouped, lo=0, hi=P):
-            copy(
-                out=grouped[:].rearrange("p (t m j) -> p m j t", t=4, j=J)[:, lo:hi],
-                in_=raw[:].rearrange("p j (m t) -> p m j t", t=4)[:, lo:hi],
-            )
-
-        def new_grouped():
-            grouped = stage.tile([P, 512 * J], BF16, name="grouped", align_bytes=64)
-            return grouped
-
-        def quantise(grouped, codes, scales):
-            nc.vector.quantize_mx(out=codes.bitcast(FP8X4), scales=scales, in_=grouped[:])
-
-        def copy_x(s, half, raw):
-            grouped = new_grouped()
-            group(nc.scalar.copy, raw, grouped, 0, 256)
-            group(nc.vector.tensor_copy, raw, grouped, 256, 512)
-            return grouped
-
-        def quant_x(s, half, grouped):
-            cols = slice(half * 512, (half + 1) * 512)
-            quantise(grouped, x_codes[s][:, cols], x_scales[4 * s : P, cols])
-
-        def gather(s):
-            nc.vector.tensor_copy(g_codes[s][:], x_codes[s][:].indirect(offsets[:]))
-
-        def copy_w1(e, s, raw):
-            grouped = new_grouped()
-            if s == 0:
-                group_turned(nc.scalar.copy, raw, grouped)
+        def load_chunk(c):
+            if c == "o":
+                nc.sync.dma_start(offsets[:], offs)
+                return
+            if c == "g":
+                nc.sync.dma_start(out=gates[:], in_=gate[0:P, :])
+                return
+            e = int(c[1])
+            if c[0] == "r":
+                nc.sync.dma_start(out=res[e][:], in_=xr[e * P : (e + 1) * P, :])
+                return
+            w = 256 if c[2:] in ("L", "R") else 512
+            if c[0] == "x":
+                h = int(c[2])
+                src = xT[e * KP : (e + 1) * KP, h * 512 : (h + 1) * 512]
+            elif c[0] == "a":
+                s = int(c[2])
+                src = w1[e][s * KP : (s + 1) * KP, :]
+            elif w == 256:
+                h = 0 if c[2] == "L" else 1
+                src = w2[e][:, h * 256 : (h + 1) * 256]
             else:
-                group_turned(nc.scalar.copy, raw, grouped, 0, P // 2)
-                group_turned(nc.vector.tensor_copy, raw, grouped, P // 2, P)
-            return grouped
+                src = w2[e]
+            t = raws.tile([P, J, w], F32, name="raw") if w == 512 else ys.tile([P, J, w], F32, name="rawh", bufs=2)
+            nc.sync.dma_start(out=t[:], in_=src.rearrange("(p j) c -> p j c", j=J))
+            raw[c] = t
 
-        def quant_w1(e, s, grouped):
-            quantise(grouped, w1_codes[e][s][:], w1_scales[e][s][:])
+        def grouped_of(c):
+            t = raw[c]
+            w = 256 if c[2:] in ("L", "R") else 512
+            g = keep.tile([P, w * J], BF16, name="grouped_" + c, align_bytes=64)
+            n4 = w // 4
+            cut = n4 - int(n4 * PARAMS["share"].get(c, 0.5))
+            if c[0] == "a":
+                o = g[:].rearrange("p (t m j) -> p m j t", t=4, j=J)
+                i = t[:].rearrange("p j (m t) -> p m j t", t=4)
+            else:
+                o = g[:].rearrange("p (c i j) -> p c j i", i=4, j=J)
+                i = t[:].rearrange("p j (c i) -> p c j i", i=4)
+            if cut > 0:
+                nc.scalar.copy(out=o[:, :cut], in_=i[:, :cut])
+            if cut < n4:
+                nc.vector.tensor_copy(out=o[:, cut:], in_=i[:, cut:])
+            return g
 
-        def do_w2(e, raw):
-            grouped = new_grouped()
-            group(nc.scalar.copy, raw, grouped)
-            quantise(grouped, w2_codes[e][:], w2_scales[e][:])
+        def quant(g, codes, scales):
+            nc.vector.quantize_mx(out=codes.bitcast(FP8X4), scales=scales, in_=g[:])
 
         def layer1(e):
             slots = slice(e * C, (e + 1) * C)
-            acc = psum.tile([P, 4, C], F32, name="acc1")
+            acc = psum.tile([P, 4, C], F32, name="acc1_" + str(e % 2))
             for t in range(4):
                 rows = slice(t * P, (t + 1) * P)
                 for s in range(PASSES):
@@ -142,34 +117,33 @@ def tile_moe_res_mlp_relu_kernel(tc, xT, xr, w1, w2, gate, offs, out):
                         start=(s == 0),
                         stop=(s == PASSES - 1),
                     )
-            hidden = work.tile([P, C * J], BF16, name="hidden", align_bytes=64)
+            hidden = keep.tile([P, C * J], BF16, name="hidden_" + str(e), align_bytes=64)
             nc.scalar.activation(
                 out=hidden[:].rearrange("p (c t) -> p c t", t=4),
                 in_=acc[:].rearrange("p t c -> p c t"),
                 func=RELU,
             )
-            h_codes = work.tile([P, C], U32, name="h_codes", align_bytes=64)
-            h_scales = work.tile([P, C], U8, name="h_scales", align_bytes=64)
-            nc.vector.quantize_mx(out=h_codes[:].bitcast(FP8X4), scales=h_scales[:], in_=hidden[:])
-            return h_codes, h_scales
+            hc = keep.tile([P, C], U32, name="h_codes_" + str(e), align_bytes=64)
+            hs = keep.tile([P, C], U8, name="h_scales_" + str(e), align_bytes=64)
+            nc.vector.quantize_mx(out=hc[:].bitcast(FP8X4), scales=hs[:], in_=hidden[:])
+            return hc, hs
 
-        def layer2(e, h, tiles=range(NT)):
-            h_codes, h_scales = h
-            acc = psum.tile([P, len(tiles), C], F32, name="acc2")
-            for i, n in enumerate(tiles):
+        def layer2(e, h, tl):
+            acc = psum.tile([P, len(tl), C], F32, name="acc2_" + str(e) + "_" + str(tl[0]))
+            for i, n in enumerate(tl):
                 rows = slice(n * P, (n + 1) * P)
                 nc.tensor.matmul_mx(
                     out=acc[:, i, :],
                     lhsT=w2_codes[e][:, rows].bitcast(FP8X4),
                     lhsT_scale=w2_scales[e][:, rows],
-                    rhs=h_codes[:].bitcast(FP8X4),
-                    rhs_scale=h_scales[:],
+                    rhs=h[0][:].bitcast(FP8X4),
+                    rhs_scale=h[1][:],
                     start=True,
                     stop=True,
                 )
-            y = ys.tile([P, len(tiles), C], F32, name="y")
+            y = keep.tile([P, len(tl), C], F32, name="y_" + str(e) + "_" + str(tl[0]))
             nc.scalar.copy(out=y[:], in_=acc[:])
-            return [y[:, i, :] for i in range(len(tiles))]
+            return [y[:, i, :] for i in range(len(tl))]
 
         def scatter(e, n, y):
             nc.vector.tensor_tensor(
@@ -179,57 +153,71 @@ def tile_moe_res_mlp_relu_kernel(tc, xT, xr, w1, w2, gate, offs, out):
                 MULT,
             )
 
-        r_x = [[None, None], [None, None]]
-        r_a = [[None, None] for e in range(E)]
-        r_b = [None for e in range(E)]
-        r_x[0][0] = load_x(0, 0)
-        r_x[0][1] = load_x(0, 1)
-        nc.sync.dma_start(offsets[:], offs)
-        r_x[1][0] = load_x(1, 0)
-        r_x[1][1] = load_x(1, 1)
-        r_a[0][0] = load_w1(0, 0)
-        r_a[0][1] = load_w1(0, 1)
-        r_b[0] = load_w2(0)
-        nc.sync.dma_start(out=gates[:], in_=gate[0:P, :])
-        for e in range(1, E):
-            r_a[e][0] = load_w1(e, 0)
-            r_a[e][1] = load_w1(e, 1)
-            if e < E - 1:
-                r_b[e] = load_w2(e)
-            else:
-                r_b[e] = [load_half_w2(e, half) for half in range(2)]
-        for n in range(NT):
-            rows = slice(n * P, (n + 1) * P)
-            nc.sync.dma_start(out=res[n][:], in_=xr[rows, :])
+        for c in PARAMS["loads"]:
+            load_chunk(c)
+        done = {}
+        hs = {}
+        y = {}
+        ready = []
 
-        for s in range(PASSES):
-            left = copy_x(s, 0, r_x[s][0])
-            right = copy_x(s, 1, r_x[s][1])
-            quant_x(s, 0, left)
-            quant_x(s, 1, right)
-            gather(s)
-        nc.vector.tensor_copy(g_scales[:], x_scales[:].indirect(offsets[:]))
-
-        y = []
-        for e in range(E):
-            g_0 = copy_w1(e, 0, r_a[e][0])
-            g_1 = copy_w1(e, 1, r_a[e][1])
-            quant_w1(e, 0, g_0)
-            quant_w1(e, 1, g_1)
-            if e < E - 1:
-                do_w2(e, r_b[e])
-                y.append(layer2(e, layer1(e)))
+        def run_chunk(c):
+            g = grouped_of(c)
+            e = int(c[1])
+            if c[0] == "x":
+                h = int(c[2])
+                cols = slice(h * 512, (h + 1) * 512)
+                quant(g, x_codes[e][:, cols], x_scales[4 * e : P, cols])
+            elif c[0] == "a":
+                quant(g, w1_codes[e][int(c[2])][:], w1_scales[e][int(c[2])][:])
             else:
-                for half in range(2):
-                    do_half_w2(e, half, r_b[e][half])
-                h = layer1(e)
-                y.append(layer2(e, h, range(2)) + layer2(e, h, range(2, 4)))
-            if e >= 1:
+                cols = {"L": slice(0, 256), "R": slice(256, 512), "": slice(0, 512)}[c[2:]]
+                quant(g, w2_codes[e][:, cols], w2_scales[e][:, cols])
+            done[c] = True
+            if c[0] == "x" and "x%d%d" % (e, 1 - int(c[2])) in done:
+                nc.vector.tensor_copy(g_codes[e][:], x_codes[e][:].indirect(offsets[:]))
+                done["G%d" % e] = True
+                if "G%d" % (1 - e) in done:
+                    nc.vector.tensor_copy(g_scales[:], x_scales[:].indirect(offsets[:]))
+                    done["G"] = True
+
+        def advance():
+            for e in range(E):
+                if "G" in done and "a%d0" % e in done and "a%d1" % e in done and e not in hs:
+                    hs[e] = layer1(e)
+                if e in hs:
+                    for k, tl in (("", [0, 1, 2, 3]), ("L", [0, 1]), ("R", [2, 3])):
+                        if "b%d%s" % (e, k) in done and (e, tl[0]) not in y:
+                            for n, v in zip(tl, layer2(e, hs[e], tl)):
+                                y[(e, n)] = v
+                                ready.append((e, n))
+
+        pend = []
+        nxt = [0] * NT
+        order = PARAMS["experts"]
+
+        def flush(limit):
+            for k, e in enumerate(order[:-1]):
                 for n in range(NT):
-                    scatter(e - 1, n, y[e - 1][n])
+                    if (e, n) in y and nxt[n] == k and limit > 0:
+                        scatter(e, n, y[(e, n)])
+                        nxt[n] += 1
+                        limit -= 1
+
+        chunks = [c for c in PARAMS["loads"] if c[0] in ("x", "a", "b")]
+        for c in chunks:
+            run_chunk(c)
+            if PARAMS["lag"] == 0:
+                advance()
+                flush(100)
+            elif PARAMS["lag"] == 1:
+                flush(PARAMS["quota"])
+                advance()
+            else:
+                advance()
+        flush(100)
         for n in range(NT):
             rows = slice(n * P, (n + 1) * P)
-            scatter(E - 1, n, y[E - 1][n])
+            scatter(order[-1], n, y[(order[-1], n)])
             parts = 1 if n < NT - 1 else 2
             for i in range(parts):
                 cols = slice(i * T // parts, (i + 1) * T // parts)

@@ -16,210 +16,259 @@ ADD = mybir.AluOpType.add
 MULT = mybir.AluOpType.mult
 RELU = mybir.ActivationFunctionType.Relu
 
-PARAMS = {"loads":["x01","o","x00","a01","x11","x10","a00","b0","a21","g","a31","b1","a10","a11","a20","b2","a30","b3R","b3L","r3","r2","r0","r1"],"share":{"x00":0.75,"x01":0.25,"x10":0.5,"x11":0.5,"a00":0,"a01":0.5,"b0":0.75,"a10":0.25,"a11":0.25,"b1":0.5,"a20":0.25,"a21":0.75,"b2":0.25,"a30":0,"a31":0,"b3L":0,"b3R":0.5},"raws":9,"stage":1,"lag":2,"quota":2,"experts":[0,1,2,3]}
-
 P = 128
 J = 4
-KP = P * J
-PASSES = K // KP
+K_PASS = P * J
+PASSES = K // K_PASS
+COLS = 512
+HALF = COLS // 2
 NT = N // P
+
+LOADS = (
+    ("xT", 0, 0),
+    ("xT", 0, 1),
+    ("offs",),
+    ("xT", 1, 0),
+    ("xT", 1, 1),
+    ("w2", 0, 0, COLS),
+    ("w1", 0, 0),
+    ("w1", 0, 1),
+    ("w1", 1, 0),
+    ("w1", 1, 1),
+    ("w2", 1, 0, COLS),
+    ("gate", 0),
+    ("w2", 2, 0, COLS),
+    ("w1", 2, 0),
+    ("w1", 2, 1),
+    ("w1", 3, 0),
+    ("gate", 1),
+    ("w1", 3, 1),
+    ("gate", 2),
+    ("w2", 3, 0, HALF),
+    ("xr", 0),
+    ("w2", 3, HALF, HALF),
+    ("gate", 3),
+    ("xr", 1),
+    ("xr", 2),
+    ("xr", 3),
+)
+
+VECTOR_EIGHTHS = {
+    ("xT", 0, 0): 7,
+    ("xT", 0, 1): 7,
+    ("xT", 1, 0): 2,
+    ("xT", 1, 1): 1,
+    ("w1", 0, 0): 0,
+    ("w1", 0, 1): 2,
+    ("w1", 1, 0): 3,
+    ("w1", 1, 1): 2,
+    ("w1", 2, 0): 4,
+    ("w1", 2, 1): 2,
+    ("w1", 3, 0): 1,
+    ("w1", 3, 1): 0,
+    ("w2", 0, 0, COLS): 6,
+    ("w2", 1, 0, COLS): 1,
+    ("w2", 2, 0, COLS): 4,
+    ("w2", 3, 0, HALF): 0,
+    ("w2", 3, HALF, HALF): 0,
+}
 
 
 def tile_moe_res_mlp_relu_kernel(tc, xT, xr, w1, w2, gate, offs, out):
     nc = tc.nc
     with ExitStack() as ctx:
         keep = ctx.enter_context(tc.tile_pool(name="keep", bufs=1))
-        raws = ctx.enter_context(tc.tile_pool(name="raws", bufs=PARAMS["raws"]))
-        stage = ctx.enter_context(tc.tile_pool(name="stage", bufs=PARAMS["stage"]))
-        work = ctx.enter_context(tc.tile_pool(name="work", bufs=4))
-        ys = ctx.enter_context(tc.tile_pool(name="ys", bufs=5))
+        big = ctx.enter_context(tc.tile_pool(name="big", bufs=2))
+        raws = ctx.enter_context(tc.tile_pool(name="raws", bufs=9))
+        halves = ctx.enter_context(tc.tile_pool(name="halves", bufs=2))
         psum = ctx.enter_context(tc.psum_pool(name="psum", bufs=1))
 
         offsets = keep.tile([P, S // 16], U16, name="offsets")
-        gates = keep.tile([P, S], F32, name="gates")
+        gates = [keep.tile([P, C], F32, name=f"gates{e}") for e in range(E)]
         x_codes = [keep.tile([P, T], U32, name=f"x_codes{s}", align_bytes=64) for s in range(PASSES)]
+        slot_codes = [keep.tile([P, S], U32, name=f"slot_codes{s}", align_bytes=64) for s in range(PASSES)]
         x_scales = keep.tile([P, T], U8, name="x_scales", align_bytes=64)
-        g_codes = [keep.tile([P, S], U32, name=f"g_codes{s}", align_bytes=64) for s in range(PASSES)]
-        g_scales = keep.tile([P, S], U8, name="g_scales", align_bytes=64)
-        w1_codes = [[keep.tile([P, H], U32, name=f"w1_codes{e}_{s}", align_bytes=64) for s in range(PASSES)] for e in range(E)]
-        w1_scales = [[keep.tile([P, H], U8, name=f"w1_scales{e}_{s}", align_bytes=64) for s in range(PASSES)] for e in range(E)]
+        slot_scales = keep.tile([P, S], U8, name="slot_scales", align_bytes=64)
+        w1_codes = [
+            [keep.tile([P, H], U32, name=f"w1_codes{e}_{s}", align_bytes=64) for s in range(PASSES)] for e in range(E)
+        ]
+        w1_scales = [
+            [keep.tile([P, H], U8, name=f"w1_scales{e}_{s}", align_bytes=64) for s in range(PASSES)] for e in range(E)
+        ]
         w2_codes = [keep.tile([P, N], U32, name=f"w2_codes{e}", align_bytes=64) for e in range(E)]
         w2_scales = [keep.tile([P, N], U8, name=f"w2_scales{e}", align_bytes=64) for e in range(E)]
         windows = [keep.tile([P, T], F32, name=f"window{n}") for n in range(NT)]
-        res = [keep.tile([P, T], F32, name=f"res{n}") for n in range(NT)]
+        x_raw = []
+        for s in range(PASSES):
+            x_tile = big.tile([P, J, T], F32, name="big")
+            x_raw.append(x_tile)
+        residual = big.tile([P, NT, T], F32, name="big")
 
+        table = keep.tile([P, 2], F32, name="table")
+        nc.vector.memset(table[:], 0.0)
+        nc.scalar.activation(out=table[:, 1:2], in_=table[:, 0:1], func=RELU)
         nc.gpsimd.memset(x_scales[:], 0)
         for n in range(NT):
             nc.gpsimd.memset(windows[n][:], 0.0)
 
-        raw = {}
+        w_raw = {}
 
-        def load_chunk(c):
-            if c == "o":
+        def rows_by_four(matrix):
+            return matrix.rearrange("(p j) c -> p j c", j=J)
+
+        def load(piece):
+            kind = piece[0]
+            if kind == "offs":
                 nc.sync.dma_start(offsets[:], offs)
-                return
-            if c == "g":
-                nc.sync.dma_start(out=gates[:], in_=gate[0:P, :])
-                return
-            e = int(c[1])
-            if c[0] == "r":
-                nc.sync.dma_start(out=res[e][:], in_=xr[e * P : (e + 1) * P, :])
-                return
-            w = 256 if c[2:] in ("L", "R") else 512
-            if c[0] == "x":
-                h = int(c[2])
-                src = xT[e * KP : (e + 1) * KP, h * 512 : (h + 1) * 512]
-            elif c[0] == "a":
-                s = int(c[2])
-                src = w1[e][s * KP : (s + 1) * KP, :]
-            elif w == 256:
-                h = 0 if c[2] == "L" else 1
-                src = w2[e][:, h * 256 : (h + 1) * 256]
+            elif kind == "gate":
+                e = piece[1]
+                nc.sync.dma_start(out=gates[e][:], in_=gate[0:P, e * C : (e + 1) * C])
+            elif kind == "xr":
+                n = piece[1]
+                nc.sync.dma_start(out=residual[:, n, :], in_=xr[n * P : (n + 1) * P, :])
+            elif kind == "xT":
+                s, half = piece[1:]
+                rows = slice(2 * half, 2 * half + 2)
+                source = rows_by_four(xT[s * K_PASS : (s + 1) * K_PASS, :])
+                nc.sync.dma_start(out=x_raw[s][:, rows, :], in_=source[:, rows, :])
+            elif kind == "w1":
+                e, s = piece[1:]
+                raw = raws.tile([P, J, COLS], F32, name="raw")
+                nc.sync.dma_start(out=raw[:], in_=rows_by_four(w1[e][s * K_PASS : (s + 1) * K_PASS, :]))
+                w_raw[piece] = raw
             else:
-                src = w2[e]
-            t = raws.tile([P, J, w], F32, name="raw") if w == 512 else ys.tile([P, J, w], F32, name="rawh", bufs=2)
-            nc.sync.dma_start(out=t[:], in_=src.rearrange("(p j) c -> p j c", j=J))
-            raw[c] = t
+                e, first, columns = piece[1:]
+                if columns == COLS:
+                    raw = raws.tile([P, J, COLS], F32, name="raw")
+                else:
+                    raw = halves.tile([P, J, HALF], F32, name="raw_half")
+                nc.sync.dma_start(out=raw[:], in_=rows_by_four(w2[e][:, first : first + columns]))
+                w_raw[piece] = raw
 
-        def grouped_of(c):
-            t = raw[c]
-            w = 256 if c[2:] in ("L", "R") else 512
-            g = keep.tile([P, w * J], BF16, name="grouped_" + c, align_bytes=64)
-            n4 = w // 4
-            cut = n4 - int(n4 * PARAMS["share"].get(c, 0.5))
-            if c[0] == "a":
-                o = g[:].rearrange("p (t m j) -> p m j t", t=4, j=J)
-                i = t[:].rearrange("p j (m t) -> p m j t", t=4)
+        def interleave(piece):
+            kind = piece[0]
+            if kind == "xT":
+                s, half = piece[1:]
+                source = x_raw[s][:, :, half * COLS : (half + 1) * COLS]
+                columns = COLS
             else:
-                o = g[:].rearrange("p (c i j) -> p c j i", i=4, j=J)
-                i = t[:].rearrange("p j (c i) -> p c j i", i=4)
+                source = w_raw[piece][:]
+                columns = piece[3] if kind == "w2" else COLS
+            if kind == "w1" and piece[1] >= 2:
+                tag = f"{piece[1] - 2}_{piece[2]}"
+            elif kind == "xT":
+                tag = f"{piece[1]}_{piece[2]}"
+            else:
+                tag = f"{kind}_{piece[1]}_{piece[2]}"
+            grouped = keep.tile([P, columns * J], BF16, name="grouped_" + tag, align_bytes=64)
+            if kind == "w1":
+                target = grouped[:].rearrange("p (t m j) -> p m j t", t=4, j=J)
+                source = source.rearrange("p j (m t) -> p m j t", t=4)
+            else:
+                target = grouped[:].rearrange("p (c i j) -> p c j i", i=4, j=J)
+                source = source.rearrange("p j (c i) -> p c j i", i=4)
+            runs = columns // 4
+            cut = runs - runs * VECTOR_EIGHTHS[piece] // 8
             if cut > 0:
-                nc.scalar.copy(out=o[:, :cut], in_=i[:, :cut])
-            if cut < n4:
-                nc.vector.tensor_copy(out=o[:, cut:], in_=i[:, cut:])
-            return g
+                nc.scalar.copy(out=target[:, :cut], in_=source[:, :cut])
+            if cut < runs:
+                nc.vector.tensor_copy(out=target[:, cut:], in_=source[:, cut:])
+            return grouped
 
-        def quant(g, codes, scales):
-            nc.vector.quantize_mx(out=codes.bitcast(FP8X4), scales=scales, in_=g[:])
+        def quantise(grouped, codes, scales):
+            nc.vector.quantize_mx(out=codes.bitcast(FP8X4), scales=scales, in_=grouped[:])
 
-        def layer1(e):
+        def first_layer(e):
             slots = slice(e * C, (e + 1) * C)
-            acc = psum.tile([P, 4, C], F32, name="acc1_" + str(e % 2))
-            for t in range(4):
-                rows = slice(t * P, (t + 1) * P)
+            acc = psum.tile([P, J, C], F32, name=f"acc1_{e % 2}")
+            for t in range(J):
+                channels = slice(t * P, (t + 1) * P)
                 for s in range(PASSES):
                     nc.tensor.matmul_mx(
                         out=acc[:, t, :],
-                        lhsT=w1_codes[e][s][:, rows].bitcast(FP8X4),
-                        lhsT_scale=w1_scales[e][s][:, rows],
-                        rhs=g_codes[s][:, slots].bitcast(FP8X4),
-                        rhs_scale=g_scales[4 * s : P, slots],
+                        lhsT=w1_codes[e][s][:, channels].bitcast(FP8X4),
+                        lhsT_scale=w1_scales[e][s][:, channels],
+                        rhs=slot_codes[s][:, slots].bitcast(FP8X4),
+                        rhs_scale=slot_scales[4 * s : P, slots],
                         start=(s == 0),
                         stop=(s == PASSES - 1),
                     )
-            hidden = keep.tile([P, C * J], BF16, name="hidden_" + str(e), align_bytes=64)
+            hidden = keep.tile([P, C * J], BF16, name=f"hidden_{e}", align_bytes=64)
             nc.scalar.activation(
-                out=hidden[:].rearrange("p (c t) -> p c t", t=4),
+                out=hidden[:].rearrange("p (c t) -> p c t", t=J),
                 in_=acc[:].rearrange("p t c -> p c t"),
                 func=RELU,
             )
-            hc = keep.tile([P, C], U32, name="h_codes_" + str(e), align_bytes=64)
-            hs = keep.tile([P, C], U8, name="h_scales_" + str(e), align_bytes=64)
-            nc.vector.quantize_mx(out=hc[:].bitcast(FP8X4), scales=hs[:], in_=hidden[:])
-            return hc, hs
+            codes = keep.tile([P, C], U32, name=f"h_codes_{e}", align_bytes=64)
+            scales = keep.tile([P, C], U8, name=f"h_scales_{e}", align_bytes=64)
+            quantise(hidden, codes[:], scales[:])
+            return codes, scales
 
-        def layer2(e, h, tl):
-            acc = psum.tile([P, len(tl), C], F32, name="acc2_" + str(e) + "_" + str(tl[0]))
-            for i, n in enumerate(tl):
+        def second_layer(e, h, tiles):
+            codes, scales = h
+            acc = psum.tile([P, len(tiles), C], F32, name=f"acc2_{e}_{tiles[0]}")
+            for i, n in enumerate(tiles):
                 rows = slice(n * P, (n + 1) * P)
                 nc.tensor.matmul_mx(
                     out=acc[:, i, :],
                     lhsT=w2_codes[e][:, rows].bitcast(FP8X4),
                     lhsT_scale=w2_scales[e][:, rows],
-                    rhs=h[0][:].bitcast(FP8X4),
-                    rhs_scale=h[1][:],
+                    rhs=codes[:].bitcast(FP8X4),
+                    rhs_scale=scales[:],
                     start=True,
                     stop=True,
                 )
-            y = keep.tile([P, len(tl), C], F32, name="y_" + str(e) + "_" + str(tl[0]))
-            nc.scalar.copy(out=y[:], in_=acc[:])
-            return [y[:, i, :] for i in range(len(tl))]
+            result = keep.tile([P, len(tiles), C], F32, name=f"y_{e}_{tiles[0]}")
+            nc.scalar.copy(out=result[:], in_=acc[:])
+            for i, n in enumerate(tiles):
+                y[(e, n)] = result[:, i, :]
 
-        def scatter(e, n, y):
+        def scatter(e, n):
             nc.vector.tensor_tensor(
                 windows[n][:].indirect(offsets[:, e * (C // 16) : (e + 1) * (C // 16)]),
-                y,
-                gates[:, e * C : (e + 1) * C],
+                y[(e, n)],
+                gates[e][:],
                 MULT,
             )
 
-        for c in PARAMS["loads"]:
-            load_chunk(c)
-        done = {}
-        hs = {}
+        for piece in LOADS:
+            load(piece)
+
+        h = {}
         y = {}
-        ready = []
+        waiting = []
+        for piece in LOADS:
+            kind = piece[0]
+            if kind == "xT":
+                s, half = piece[1:]
+                tokens = slice(half * COLS, (half + 1) * COLS)
+                quantise(interleave(piece), x_codes[s][:, tokens], x_scales[4 * s : P, tokens])
+                if half == 1:
+                    nc.vector.tensor_copy(slot_codes[s][:], x_codes[s][:].indirect(offsets[:]))
+                    if s == PASSES - 1:
+                        nc.vector.tensor_copy(slot_scales[:], x_scales[:].indirect(offsets[:]))
+            elif kind == "w1":
+                e, s = piece[1:]
+                quantise(interleave(piece), w1_codes[e][s][:], w1_scales[e][s][:])
+                if s == PASSES - 1:
+                    h[e] = first_layer(e)
+            elif kind == "w2":
+                e, first, columns = piece[1:]
+                rows = slice(first, first + columns)
+                quantise(interleave(piece), w2_codes[e][:, rows], w2_scales[e][:, rows])
+                waiting.append((e, range(first // P, (first + columns) // P)))
+            for e, tiles in list(waiting):
+                if e in h:
+                    second_layer(e, h[e], tiles)
+                    waiting.remove((e, tiles))
 
-        def run_chunk(c):
-            g = grouped_of(c)
-            e = int(c[1])
-            if c[0] == "x":
-                h = int(c[2])
-                cols = slice(h * 512, (h + 1) * 512)
-                quant(g, x_codes[e][:, cols], x_scales[4 * e : P, cols])
-            elif c[0] == "a":
-                quant(g, w1_codes[e][int(c[2])][:], w1_scales[e][int(c[2])][:])
-            else:
-                cols = {"L": slice(0, 256), "R": slice(256, 512), "": slice(0, 512)}[c[2:]]
-                quant(g, w2_codes[e][:, cols], w2_scales[e][:, cols])
-            done[c] = True
-            if c[0] == "x" and "x%d%d" % (e, 1 - int(c[2])) in done:
-                nc.vector.tensor_copy(g_codes[e][:], x_codes[e][:].indirect(offsets[:]))
-                done["G%d" % e] = True
-                if "G%d" % (1 - e) in done:
-                    nc.vector.tensor_copy(g_scales[:], x_scales[:].indirect(offsets[:]))
-                    done["G"] = True
-
-        def advance():
-            for e in range(E):
-                if "G" in done and "a%d0" % e in done and "a%d1" % e in done and e not in hs:
-                    hs[e] = layer1(e)
-                if e in hs:
-                    for k, tl in (("", [0, 1, 2, 3]), ("L", [0, 1]), ("R", [2, 3])):
-                        if "b%d%s" % (e, k) in done and (e, tl[0]) not in y:
-                            for n, v in zip(tl, layer2(e, hs[e], tl)):
-                                y[(e, n)] = v
-                                ready.append((e, n))
-
-        pend = []
-        nxt = [0] * NT
-        order = PARAMS["experts"]
-
-        def flush(limit):
-            for k, e in enumerate(order[:-1]):
-                for n in range(NT):
-                    if (e, n) in y and nxt[n] == k and limit > 0:
-                        scatter(e, n, y[(e, n)])
-                        nxt[n] += 1
-                        limit -= 1
-
-        chunks = [c for c in PARAMS["loads"] if c[0] in ("x", "a", "b")]
-        for c in chunks:
-            run_chunk(c)
-            if PARAMS["lag"] == 0:
-                advance()
-                flush(100)
-            elif PARAMS["lag"] == 1:
-                flush(PARAMS["quota"])
-                advance()
-            else:
-                advance()
-        flush(100)
+        for e in range(E - 1):
+            for n in range(NT):
+                scatter(e, n)
         for n in range(NT):
             rows = slice(n * P, (n + 1) * P)
-            scatter(order[-1], n, y[(order[-1], n)])
-            parts = 1 if n < NT - 1 else 2
-            for i in range(parts):
-                cols = slice(i * T // parts, (i + 1) * T // parts)
-                nc.vector.tensor_tensor(res[n][:, cols], windows[n][:, cols], res[n][:, cols], ADD)
-                nc.sync.dma_start(out=out[rows, cols], in_=res[n][:, cols])
+            scatter(E - 1, n)
+            for half in range(2):
+                tokens = slice(half * T // 2, (half + 1) * T // 2)
+                nc.vector.tensor_tensor(residual[:, n, tokens], windows[n][:, tokens], residual[:, n, tokens], ADD)
+                nc.sync.dma_start(out=out[rows, tokens], in_=residual[:, n, tokens])

from contextlib import ExitStack

import concourse.mybir as mybir

K, T, E, C, H, N = 1024, 1024, 4, 128, 512, 512
S = E * C
FLOPS = 2 * S * (K * H + H * N)

F32 = mybir.dt.float32
BF16 = mybir.dt.bfloat16
U32 = mybir.dt.uint32
U16 = mybir.dt.uint16
U8 = mybir.dt.uint8
FP8X4 = mybir.dt.float8_e4m3fn_x4
ADD = mybir.AluOpType.add
MULT = mybir.AluOpType.mult
RELU = mybir.ActivationFunctionType.Relu

P = 128
J = 4
K_PASS = P * J
PASSES = K // K_PASS
COLS = 512
HALF = COLS // 2
NT = N // P

LOADS = (
    ("xT", 0, 0),
    ("xT", 0, 1),
    ("offs",),
    ("xT", 1, 0),
    ("xT", 1, 1),
    ("w2", 0, 0, COLS),
    ("w1", 0, 0),
    ("w1", 0, 1),
    ("w1", 1, 0),
    ("w1", 1, 1),
    ("w2", 1, 0, COLS),
    ("gate", 0),
    ("w2", 2, 0, COLS),
    ("w1", 2, 0),
    ("w1", 2, 1),
    ("w1", 3, 0),
    ("gate", 1),
    ("w1", 3, 1),
    ("gate", 2),
    ("w2", 3, 0, HALF),
    ("xr", 0),
    ("w2", 3, HALF, HALF),
    ("gate", 3),
    ("xr", 1),
    ("xr", 2),
    ("xr", 3),
)

VECTOR_EIGHTHS = {
    ("xT", 0, 0): 7,
    ("xT", 0, 1): 7,
    ("xT", 1, 0): 2,
    ("xT", 1, 1): 1,
    ("w1", 0, 0): 0,
    ("w1", 0, 1): 2,
    ("w1", 1, 0): 3,
    ("w1", 1, 1): 2,
    ("w1", 2, 0): 4,
    ("w1", 2, 1): 2,
    ("w1", 3, 0): 1,
    ("w1", 3, 1): 0,
    ("w2", 0, 0, COLS): 6,
    ("w2", 1, 0, COLS): 1,
    ("w2", 2, 0, COLS): 4,
    ("w2", 3, 0, HALF): 0,
    ("w2", 3, HALF, HALF): 0,
}


def tile_moe_res_mlp_relu_kernel(tc, xT, xr, w1, w2, gate, offs, out):
    nc = tc.nc
    with ExitStack() as ctx:
        keep = ctx.enter_context(tc.tile_pool(name="keep", bufs=1))
        big = ctx.enter_context(tc.tile_pool(name="big", bufs=2))
        raws = ctx.enter_context(tc.tile_pool(name="raws", bufs=9))
        halves = ctx.enter_context(tc.tile_pool(name="halves", bufs=2))
        psum = ctx.enter_context(tc.psum_pool(name="psum", bufs=1))

        offsets = keep.tile([P, S // 16], U16, name="offsets")
        gates = [keep.tile([P, C], F32, name=f"gates{e}") for e in range(E)]
        x_codes = [keep.tile([P, T], U32, name=f"x_codes{s}", align_bytes=64) for s in range(PASSES)]
        slot_codes = [keep.tile([P, S], U32, name=f"slot_codes{s}", align_bytes=64) for s in range(PASSES)]
        x_scales = keep.tile([P, T], U8, name="x_scales", align_bytes=64)
        slot_scales = keep.tile([P, S], U8, name="slot_scales", align_bytes=64)
        w1_codes = [
            [keep.tile([P, H], U32, name=f"w1_codes{e}_{s}", align_bytes=64) for s in range(PASSES)] for e in range(E)
        ]
        w1_scales = [
            [keep.tile([P, H], U8, name=f"w1_scales{e}_{s}", align_bytes=64) for s in range(PASSES)] for e in range(E)
        ]
        w2_codes = [keep.tile([P, N], U32, name=f"w2_codes{e}", align_bytes=64) for e in range(E)]
        w2_scales = [keep.tile([P, N], U8, name=f"w2_scales{e}", align_bytes=64) for e in range(E)]
        windows = [keep.tile([P, T], F32, name=f"window{n}") for n in range(NT)]
        x_raw = []
        for s in range(PASSES):
            x_tile = big.tile([P, J, T], F32, name="big")
            x_raw.append(x_tile)
        residual = big.tile([P, NT, T], F32, name="big")

        table = keep.tile([P, 2], F32, name="table")
        nc.vector.memset(table[:], 0.0)
        nc.scalar.activation(out=table[:, 1:2], in_=table[:, 0:1], func=RELU)
        nc.gpsimd.memset(x_scales[:], 0)
        for n in range(NT):
            nc.gpsimd.memset(windows[n][:], 0.0)

        w_raw = {}

        def rows_by_four(matrix):
            return matrix.rearrange("(p j) c -> p j c", j=J)

        def load(piece):
            kind = piece[0]
            if kind == "offs":
                nc.sync.dma_start(offsets[:], offs)
            elif kind == "gate":
                e = piece[1]
                nc.sync.dma_start(out=gates[e][:], in_=gate[0:P, e * C : (e + 1) * C])
            elif kind == "xr":
                n = piece[1]
                nc.sync.dma_start(out=residual[:, n, :], in_=xr[n * P : (n + 1) * P, :])
            elif kind == "xT":
                s, half = piece[1:]
                rows = slice(2 * half, 2 * half + 2)
                source = rows_by_four(xT[s * K_PASS : (s + 1) * K_PASS, :])
                nc.sync.dma_start(out=x_raw[s][:, rows, :], in_=source[:, rows, :])
            elif kind == "w1":
                e, s = piece[1:]
                raw = raws.tile([P, J, COLS], F32, name="raw")
                nc.sync.dma_start(out=raw[:], in_=rows_by_four(w1[e][s * K_PASS : (s + 1) * K_PASS, :]))
                w_raw[piece] = raw
            else:
                e, first, columns = piece[1:]
                if columns == COLS:
                    raw = raws.tile([P, J, COLS], F32, name="raw")
                else:
                    raw = halves.tile([P, J, HALF], F32, name="raw_half")
                nc.sync.dma_start(out=raw[:], in_=rows_by_four(w2[e][:, first : first + columns]))
                w_raw[piece] = raw

        def interleave(piece):
            kind = piece[0]
            if kind == "xT":
                s, half = piece[1:]
                source = x_raw[s][:, :, half * COLS : (half + 1) * COLS]
                columns = COLS
            else:
                source = w_raw[piece][:]
                columns = piece[3] if kind == "w2" else COLS
            if kind == "w1" and piece[1] >= 2:
                tag = f"{piece[1] - 2}_{piece[2]}"
            elif kind == "xT":
                tag = f"{piece[1]}_{piece[2]}"
            else:
                tag = f"{kind}_{piece[1]}_{piece[2]}"
            grouped = keep.tile([P, columns * J], BF16, name="grouped_" + tag, align_bytes=64)
            if kind == "w1":
                target = grouped[:].rearrange("p (t m j) -> p m j t", t=4, j=J)
                source = source.rearrange("p j (m t) -> p m j t", t=4)
            else:
                target = grouped[:].rearrange("p (c i j) -> p c j i", i=4, j=J)
                source = source.rearrange("p j (c i) -> p c j i", i=4)
            runs = columns // 4
            cut = runs - runs * VECTOR_EIGHTHS[piece] // 8
            if cut > 0:
                nc.scalar.copy(out=target[:, :cut], in_=source[:, :cut])
            if cut < runs:
                nc.vector.tensor_copy(out=target[:, cut:], in_=source[:, cut:])
            return grouped

        def quantise(grouped, codes, scales):
            nc.vector.quantize_mx(out=codes.bitcast(FP8X4), scales=scales, in_=grouped[:])

        def first_layer(e):
            slots = slice(e * C, (e + 1) * C)
            acc = psum.tile([P, J, C], F32, name=f"acc1_{e % 2}")
            for t in range(J):
                channels = slice(t * P, (t + 1) * P)
                for s in range(PASSES):
                    nc.tensor.matmul_mx(
                        out=acc[:, t, :],
                        lhsT=w1_codes[e][s][:, channels].bitcast(FP8X4),
                        lhsT_scale=w1_scales[e][s][:, channels],
                        rhs=slot_codes[s][:, slots].bitcast(FP8X4),
                        rhs_scale=slot_scales[4 * s : P, slots],
                        start=(s == 0),
                        stop=(s == PASSES - 1),
                    )
            hidden = keep.tile([P, C * J], BF16, name=f"hidden_{e}", align_bytes=64)
            nc.scalar.activation(
                out=hidden[:].rearrange("p (c t) -> p c t", t=J),
                in_=acc[:].rearrange("p t c -> p c t"),
                func=RELU,
            )
            codes = keep.tile([P, C], U32, name=f"h_codes_{e}", align_bytes=64)
            scales = keep.tile([P, C], U8, name=f"h_scales_{e}", align_bytes=64)
            quantise(hidden, codes[:], scales[:])
            return codes, scales

        def second_layer(e, h, tiles):
            codes, scales = h
            acc = psum.tile([P, len(tiles), C], F32, name=f"acc2_{e}_{tiles[0]}")
            for i, n in enumerate(tiles):
                rows = slice(n * P, (n + 1) * P)
                nc.tensor.matmul_mx(
                    out=acc[:, i, :],
                    lhsT=w2_codes[e][:, rows].bitcast(FP8X4),
                    lhsT_scale=w2_scales[e][:, rows],
                    rhs=codes[:].bitcast(FP8X4),
                    rhs_scale=scales[:],
                    start=True,
                    stop=True,
                )
            result = keep.tile([P, len(tiles), C], F32, name=f"y_{e}_{tiles[0]}")
            nc.scalar.copy(out=result[:], in_=acc[:])
            for i, n in enumerate(tiles):
                y[(e, n)] = result[:, i, :]

        def scatter(e, n):
            nc.vector.tensor_tensor(
                windows[n][:].indirect(offsets[:, e * (C // 16) : (e + 1) * (C // 16)]),
                y[(e, n)],
                gates[e][:],
                MULT,
            )

        for piece in LOADS:
            load(piece)

        h = {}
        y = {}
        waiting = []
        for piece in LOADS:
            kind = piece[0]
            if kind == "xT":
                s, half = piece[1:]
                tokens = slice(half * COLS, (half + 1) * COLS)
                quantise(interleave(piece), x_codes[s][:, tokens], x_scales[4 * s : P, tokens])
                if half == 1:
                    nc.vector.tensor_copy(slot_codes[s][:], x_codes[s][:].indirect(offsets[:]))
                    if s == PASSES - 1:
                        nc.vector.tensor_copy(slot_scales[:], x_scales[:].indirect(offsets[:]))
            elif kind == "w1":
                e, s = piece[1:]
                quantise(interleave(piece), w1_codes[e][s][:], w1_scales[e][s][:])
                if s == PASSES - 1:
                    h[e] = first_layer(e)
            elif kind == "w2":
                e, first, columns = piece[1:]
                rows = slice(first, first + columns)
                quantise(interleave(piece), w2_codes[e][:, rows], w2_scales[e][:, rows])
                waiting.append((e, range(first // P, (first + columns) // P)))
            for e, tiles in list(waiting):
                if e in h:
                    second_layer(e, h[e], tiles)
                    waiting.remove((e, tiles))

        for e in range(E - 1):
            for n in range(NT):
                scatter(e, n)
        for n in range(NT):
            rows = slice(n * P, (n + 1) * P)
            scatter(E - 1, n)
            for half in range(2):
                tokens = slice(half * T // 2, (half + 1) * T // 2)
                nc.vector.tensor_tensor(residual[:, n, tokens], windows[n][:, tokens], residual[:, n, tokens], ADD)
                nc.sync.dma_start(out=out[rows, tokens], in_=residual[:, n, tokens])
